import numpy as np
import ml_dtypes


def mxq(x, axis, fmt="e4m3"):
    dtype, down = {"e4m3": (ml_dtypes.float8_e4m3fn, 7), "e5m2": (ml_dtypes.float8_e5m2, 14)}[fmt]
    v = np.moveaxis(np.asarray(x, np.float32).astype(ml_dtypes.bfloat16).astype(np.float64), axis, -1)
    blocks = v.reshape(v.shape[:-1] + (-1, 32))
    amax = np.abs(blocks).max(-1, keepdims=True)
    byte = np.maximum(np.where(amax > 0, np.frexp(amax)[1] - 1 + 127, 0) - down, 1)
    scale = np.exp2(byte - 127.0)
    codes = (blocks / scale).astype(np.float32).astype(dtype).astype(np.float64)
    return np.moveaxis((codes * scale).reshape(v.shape), -1, axis)


WIDE = False


def mx_kscale(k):
    if not WIDE:
        return np.ones(k)
    levels = np.array([10, -10, 5, -5, 0])
    if k % 512:
        return np.exp2(np.random.permutation(np.resize(levels, k // 32))).repeat(32)
    a = np.empty((k // 512, 16))
    for p in range(k // 512):
        a[p, :8] = np.random.permutation(np.resize(levels, 8))
        for g in range(8):
            far = levels[np.abs(levels - a[p, g]) >= 10]
            a[p, g + 8] = far[np.random.randint(len(far))]
    return np.exp2(a.ravel()).repeat(32)


def f64(x):
    return np.asarray(x).astype(np.float64)


def striped(idx):
    return np.tile(idx.reshape(-1, 16).T, (8, 1)).astype(np.uint16)


def unstriped(offs):
    return offs[:16].T.reshape(-1).astype(np.int64)


E2M1 = np.array([0.0, 0.5, 1.0, 1.5, 2.0, 3.0, 4.0, 6.0, -0.0, -0.5, -1.0, -1.5, -2.0, -3.0, -4.0, -6.0])


def pack_weight(w, fmt):
    k, n = w.shape
    w = f64(np.asarray(w, np.float32).astype(ml_dtypes.bfloat16)).reshape(k // 32, 32, n)
    amax = np.abs(w).max(1)
    if fmt == "e4m3":
        byte = np.frexp(amax)[1] - 1 + 127 - 7
    else:
        mant, ex = np.frexp(amax / 6.0)
        byte = np.where(mant > 0.5, ex, ex - 1) + 127
    byte = np.clip(np.where(amax > 0, byte, 1), 1, 254)
    scaled = (w * np.exp2(127.0 - byte)[:, None, :]).reshape(k, n).astype(np.float32)
    by_word = np.ascontiguousarray(scaled.reshape(k // 512, 128, 4, n).transpose(0, 1, 3, 2))
    if fmt == "e4m3":
        words = by_word.astype(ml_dtypes.float8_e4m3fn).view(np.uint8)
    else:
        c = by_word.astype(ml_dtypes.float4_e2m1fn).view(np.uint8) & 0xF
        words = (c[..., 0::2] | (c[..., 1::2] << 4)).reshape(k // 512, 128, 2 * n)
    return np.ascontiguousarray(words), np.ascontiguousarray(byte.astype(np.uint8).reshape(k // 512, 16, n))


def unpack_weight(words, scales, fmt):
    g, _, n = scales.shape
    words = np.ascontiguousarray(words).reshape(g, 128, n, -1)
    if fmt == "e4m3":
        vals = words.view(ml_dtypes.float8_e4m3fn).astype(np.float64)
    else:
        nib = np.empty((g, 128, n, 4), np.uint8)
        nib[..., 0::2] = words & 0xF
        nib[..., 1::2] = words >> 4
        vals = E2M1[nib]
    vals = vals * np.repeat(np.exp2(scales.astype(np.float64) - 127.0), 8, axis=1)[..., None]
    return vals.transpose(0, 1, 3, 2).reshape(g * 512, n)


def gelu(v):
    return 0.5 * v * (1.0 + np.tanh(np.sqrt(2.0 / np.pi) * (v + 0.044715 * v**3)))


K, H, T, S, S2 = 1024, 512, 4096, 1024, 512


def setup_inputs():
    n = np.random.standard_normal
    s = mx_kscale(K)[:, None]
    u = mx_kscale(H)[:, None]
    d = {}
    d["tab_words"], d["tab_scales"] = pack_weight(n((K, T)) * s, "e4m3")
    d["offs"] = striped(np.random.permutation(T)[:S])
    d["offs2"] = striped(np.random.permutation(T)[:S2])
    d["w1"] = (n((K, K)) / K / s / s.T).astype(np.float32)
    d["w2_words"], d["w2_scales"] = pack_weight(n((K, H)) / K**0.5 / s * u.T, "e2m1")
    d["w3"] = (1.2 * n((H, S2)) / H**0.5 / u).astype(np.float32)
    return d


def reference(tab_words, tab_scales, offs, offs2, w1, w2_words, w2_scales, w3):
    TW = unpack_weight(tab_words, tab_scales, "e4m3")
    v = TW[:, unstriped(offs)]
    v2 = TW[:, unstriped(offs2)]
    w1q = mxq(f64(w1), 0, "e4m3")
    w2q = unpack_weight(w2_words, w2_scales, "e2m1")
    w3q = mxq(f64(w3), 0, "e4m3")
    h = np.abs(w1q.T @ v)
    e = v2.T @ mxq(h, 0, "e4m3")
    h2 = np.maximum(w2q.T @ v, 0.0)
    e2 = w3q.T @ mxq(h2, 0, "e4m3")
    return 1.0 / (1.0 + np.square(e - e2))

@@ -1,0 +1,289 @@
+from contextlib import ExitStack
+
+import concourse.mybir as mybir
+
+K, H, T, S, S2 = 1024, 512, 4096, 1024, 512
+FLOPS = 2 * S * (K * K + S2 * K + K * H + H * S2)
+
+F32 = mybir.dt.float32
+BF16 = mybir.dt.bfloat16
+I32 = mybir.dt.int32
+U32 = mybir.dt.uint32
+U16 = mybir.dt.uint16
+U8 = mybir.dt.uint8
+E4M3 = mybir.dt.float8_e4m3fn_x4
+E2M1 = mybir.dt.float4_e2m1fn_x4
+ACT = mybir.ActivationFunctionType
+ALU = mybir.AluOpType
+
+P = 128
+PACK = 4
+KP = 512
+NB = 128
+NQ = 256
+SQUARE_ON_VECTOR = (3, 5, 7)
+GS = 512
+
+
+def tile_list_stone_seating_scores_kernel(
+    tc, tab_words, tab_scales, offs, offs2, w1, w2_words, w2_scales, w3, out
+):
+    nc = tc.nc
+    with ExitStack() as ctx:
+        keep = ctx.enter_context(tc.tile_pool(name="keep", bufs=1))
+        ring = ctx.enter_context(tc.tile_pool(name="ring", bufs=3))
+        psum = ctx.enter_context(tc.psum_pool(name="psum", bufs=8))
+
+        def held(name, shape, dtype, tag=None):
+            return keep.tile(shape, dtype, name=name, tag=tag or name, align_bytes=64)
+
+        list1 = keep.tile([P, S // 16], U16, name="list1")
+        list2 = keep.tile([P, S2 // 16], U16, name="list2")
+        tab = [held("tab%d" % a, [P, T], U32) for a in range(2)]
+        tab_s = held("tab_s", [P, T], U8)
+        v = [held("v%d" % a, [P, S], U32) for a in range(2)]
+        v_s = held("v_s", [P, S], U8)
+        v_s1 = held("v_s1", [P, S], U8)
+        v2_0 = held("v2_0", [P, S2], U32)
+        v2_s = held("v2_s", [P, S2], U8)
+        w2_raw = held("w2_raw", [P, 2 * H // 2], U32)
+        w2_c = held("w2_c", [P, 2 * H // 2], U32)
+        w2_sraw = held("w2_sraw", [P, 2 * H // 4], U32)
+        w2_s = held("w2_s", [P, 2 * H // 4], U32)
+        w1_raw = {}
+        w1_c = {}
+        w1_s = {}
+        for b in range(2):
+            for a in range(2):
+                w1_raw[a, b] = held("w1_raw%d%d" % (a, b), [P, PACK, KP], F32)
+                w1_c[a, b] = held("w1_c%d%d" % (a, b), [P, KP], U32)
+                w1_s[a, b] = held("w1_s%d%d" % (a, b), [P, KP], U8)
+        w3_raw = held("w3_raw", [P, PACK, S2], F32)
+        w3_c = held("w3_c", [P, S2], U32)
+        w3_s = held("w3_s", [P, S2], U8)
+        names = ("h0", "h1", "h2")
+        h_bf = {n: held(n + "_bf", [P, PACK * S], BF16) for n in names}
+        h_c = {"h1": held("h1_c", [P, S], U32)}
+        v2_1 = {}
+        h_s = {n: held(n + "_s", [P, S], U8) for n in names}
+
+        nc.vector.memset(tab_s[:].bitcast(I32), 0)
+        nc.vector.memset(v_s1[:].bitcast(I32), 0)
+        nc.vector.memset(w2_s[:].bitcast(I32), 0)
+        for q in range(2):
+            for a in range(2):
+                nc.scalar.dma_start(
+                    out=tab_s[32 * q + 4 * a : 32 * q + 4 * a + 4, :].bitcast(I32),
+                    in_=tab_scales[a, 4 * q : 4 * q + 4, :].bitcast(I32),
+                )
+        for q in range(2, 4):
+            nc.gpsimd.dma_start(
+                out=tab_s[32 * q : 32 * q + 8, :].bitcast(I32),
+                in_=tab_scales[:, 4 * q : 4 * q + 4, :].bitcast(I32),
+            )
+
+        def load_tab(a):
+            nc.sync.dma_start(
+                out=tab[a][:].bitcast(I32), in_=tab_words[a].rearrange("p n t -> p (n t)").bitcast(I32)
+            )
+
+        nc.sync.dma_start(list1[:], offs)
+        nc.sync.dma_start(list2[:], offs2)
+        nc.sync.dma_start(
+            out=w2_raw[:].bitcast(I32).rearrange("p (a n) -> p a n", a=2),
+            in_=w2_words.bitcast(I32).rearrange("a p n -> p a n"),
+        )
+        for q in range(4):
+            nc.gpsimd.dma_start(
+                out=w2_sraw[32 * q : 32 * q + 4, :].bitcast(I32).rearrange("p (a n) -> p a n", a=2),
+                in_=w2_scales[:, 4 * q : 4 * q + 4, :].bitcast(I32).rearrange("a r n -> r a n"),
+            )
+        load_tab(0)
+        load_tab(1)
+        for b in range(2):
+            for a in range(2):
+                nc.sync.dma_start(
+                    out=w1_raw[a, b][:],
+                    in_=w1[KP * a : KP * (a + 1), KP * b : KP * (b + 1)].rearrange("(p j) c -> p j c", j=PACK),
+                )
+        w3_rows = w3.rearrange("(g t q) m -> t g q m", t=PACK, q=8)
+        for t in range(PACK):
+            nc.sync.dma_start(out=w3_raw[:, t, :], in_=w3_rows[t])
+
+        def gather_words(a):
+            for s0 in range(0, S, GS):
+                nc.vector.tensor_copy(
+                    v[a][:, s0 : s0 + GS], tab[a][:].indirect(list1[:, s0 // 16 : (s0 + GS) // 16])
+                )
+
+        nc.vector.tensor_copy(v_s[:], tab_s[:].indirect(list1[:]))
+        for r in range(4):
+            nc.scalar.dma_start(
+                out=v_s1[r:P:32, :].bitcast(I32), in_=v_s[4 + r : P : 32, :].bitcast(I32)
+            )
+        nc.vector.tensor_copy(v2_s[:], tab_s[:].indirect(list2[:]))
+        gather_words(0)
+        nc.vector.tensor_copy(v2_0[:], tab[0][:].indirect(list2[:]))
+
+        nc.scalar.copy(
+            out=w2_c[:].rearrange("p (a t g w) -> p a t g w", a=2, t=PACK, w=4),
+            in_=w2_raw[:].rearrange("p (a g t w) -> p a t g w", a=2, t=PACK, w=4),
+        )
+        for q in range(4):
+            rows = slice(32 * q, 32 * q + 4)
+            nc.scalar.copy(
+                out=w2_s[rows, :].rearrange("p (a t g w) -> p a t g w", a=2, t=PACK, w=2),
+                in_=w2_sraw[rows, :].rearrange("p (a g t w) -> p a t g w", a=2, t=PACK, w=2),
+            )
+        w2_c8 = w2_c[:].bitcast(U8)
+        w2_s8 = w2_s[:].bitcast(U8)
+
+        def quantise(codes, scales, values):
+            nc.vector.quantize_mx(out=codes.bitcast(E4M3), scales=scales, in_=values)
+
+        def prepare_w1(a, b):
+            g = held("w1_bf%d%d" % (a, b), [P, PACK * KP], BF16)
+            nc.vector.tensor_copy(
+                out=g[:].rearrange("p (t m j) -> p m j t", t=PACK, j=PACK),
+                in_=w1_raw[a, b][:].rearrange("p j (m t) -> p m j t", t=PACK),
+            )
+            return g
+
+        def first_pass(name, a, jb, bank):
+            cols = slice(NB * jb, NB * (jb + 1))
+            for t in range(PACK):
+                if name == "h2":
+                    c0 = a * H + t * P
+                    lhs = w2_c8[:, 2 * c0 : 2 * (c0 + P)].bitcast(E2M1)
+                    lhs_s = w2_s8[:, c0 : c0 + P]
+                    rhs_s = (v_s, v_s1)[a][:, cols]
+                else:
+                    b = names.index(name)
+                    lhs = w1_c[a, b][:, t * P : (t + 1) * P].bitcast(E4M3)
+                    lhs_s = w1_s[a, b][:, t * P : (t + 1) * P]
+                    rhs_s = v_s[4 * a : P, cols]
+                nc.tensor.matmul_mx(
+                    out=bank[:, t * NB : (t + 1) * NB],
+                    lhsT=lhs,
+                    lhsT_scale=lhs_s,
+                    rhs=v[a][:, cols].bitcast(E4M3),
+                    rhs_scale=rhs_s,
+                    start=(a == 0 and t == 0),
+                    stop=(a == 1 and t == PACK - 1),
+                )
+
+        def empty_first(name, jb, bank):
+            nc.scalar.activation(
+                out=h_bf[name][:, PACK * NB * jb : PACK * NB * (jb + 1)].rearrange("p (n t) -> p n t", t=PACK),
+                in_=bank[:].rearrange("p (t n) -> p n t", t=PACK),
+                func=ACT.Relu if name == "h2" else ACT.Abs,
+            )
+
+        def quantise_h(name, q):
+            cols = slice(NQ * q, NQ * (q + 1))
+            quantise(h_c[name][:, cols], h_s[name][:, cols], h_bf[name][:, PACK * NQ * q : PACK * NQ * (q + 1)])
+
+        def new_bank():
+            return psum.tile([P, 512], F32, name="bank")
+
+        def second_stage(q, half):
+            cols = slice(NQ * q, NQ * (q + 1))
+            bank = new_bank()
+            for i, name in enumerate(names):
+                for u in range(2):
+                    m = slice(P * (2 * half + u), P * (2 * half + u + 1))
+                    if name == "h2":
+                        lhs, lhs_s = w3_c[:, m], w3_s[:, m]
+                    elif name == "h0":
+                        lhs, lhs_s = v2_0[:, m], v2_s[:, m]
+                    else:
+                        lhs, lhs_s = v2_1[half][:, P * u : P * (u + 1)], v2_s[4:P, m]
+                    nc.tensor.matmul_mx(
+                        out=bank[:, u * NQ : (u + 1) * NQ],
+                        lhsT=lhs.bitcast(E4M3),
+                        lhsT_scale=lhs_s,
+                        rhs=h_c[name][:, cols].bitcast(E4M3),
+                        rhs_scale=h_s[name][:, cols],
+                        start=(i == 0 and u == 0),
+                        stop=(i == 2 and u == 1),
+                    )
+            y = ring.tile([P, 512], F32, name="y")
+            if 2 * q + half in SQUARE_ON_VECTOR:
+                d = ring.tile([P, 512], F32, name="d")
+                nc.vector.tensor_copy(d[:], bank[:])
+                nc.vector.tensor_tensor(y[:], bank[:], d[:], ALU.mult)
+            else:
+                nc.scalar.activation(out=y[:], in_=bank[:], func=ACT.Square)
+            r = ring.tile([P, 512], F32, name="r")
+            nc.scalar.activation(out=r[:], in_=y[:], func=ACT.Abs_reciprocal_sqrt, bias=1.0)
+            res = ring.tile([P, 512], F32, name="res")
+            nc.vector.tensor_tensor(res[:], r[:], r[:], ALU.mult)
+            nc.sync.dma_start(
+                out=out[2 * P * half : 2 * P * (half + 1), cols].rearrange("(u p) j -> p u j", u=2),
+                in_=res[:].rearrange("p (u j) -> p u j", u=2),
+            )
+
+        nblk = S // NB
+        banks = [new_bank() for jb in range(nblk)]
+        for jb in range(nblk):
+            first_pass("h2", 0, jb, banks[jb])
+        gather_words(1)
+        for jb in range(nblk):
+            first_pass("h2", 1, jb, banks[jb])
+            empty_first("h2", jb, banks[jb])
+
+        def gather_v2_1(half, tag):
+            v2_1[half] = held("v2_1%d" % half, [P, 2 * P], U32, tag=tag)
+            nc.vector.tensor_copy(v2_1[half][:], tab[1][:].indirect(list2[:, 16 * half : 16 * (half + 1)]))
+
+        g00 = prepare_w1(0, 0)
+        quantise(w1_c[0, 0][:], w1_s[0, 0][:], g00[:])
+        g10 = prepare_w1(1, 0)
+        quantise(w1_c[1, 0][:], w1_s[1, 0][:], g10[:])
+        gather_v2_1(0, "w1_raw10")
+
+        banks = [new_bank() for jb in range(nblk)]
+        for jb in range(nblk):
+            first_pass("h0", 0, jb, banks[jb])
+        for jb in range(nblk):
+            first_pass("h0", 1, jb, banks[jb])
+            empty_first("h0", jb, banks[jb])
+
+        g01 = prepare_w1(0, 1)
+        quantise(w1_c[0, 1][:], w1_s[0, 1][:], g01[:])
+        gather_v2_1(1, "w1_raw01")
+        g11 = prepare_w1(1, 1)
+        quantise(w1_c[1, 1][:], w1_s[1, 1][:], g11[:])
+        g3 = held("w3_bf", [P, PACK * S2], BF16)
+        nc.vector.tensor_scalar(
+            out=g3[:].rearrange("p (c i t) -> p c t i", i=4, t=PACK),
+            in0=w3_raw[:].rearrange("p t (c i) -> p c t i", i=4),
+            scalar1=-1.0,
+            scalar2=None,
+            op0=ALU.mult,
+        )
+        quantise(w3_c[:], w3_s[:], g3[:])
+        h_c["h0"] = held("h0_c", [P, S], U32, tag="w1_raw11")
+        h_c["h2"] = held("h2_c", [P, S], U32, tag="w1_bf11")
+        for q in range(4):
+            quantise_h("h0", q)
+            quantise_h("h2", q)
+
+        ahead = 6
+        banks = {}
+        for jb in range(ahead):
+            banks[jb] = new_bank()
+            first_pass("h1", 0, jb, banks[jb])
+        for q in range(4):
+            for jb in (2 * q, 2 * q + 1):
+                if jb >= ahead:
+                    banks[jb] = new_bank()
+                    first_pass("h1", 0, jb, banks[jb])
+                first_pass("h1", 1, jb, banks[jb])
+                empty_first("h1", jb, banks[jb])
+            quantise_h("h1", q)
+            if q > 0:
+                second_stage(q - 1, 0)
+                second_stage(q - 1, 1)
+        second_stage(3, 0)
+        second_stage(3, 1)

@@ -18,11 +18,16 @@ ALU = mybir.AluOpType
 
 P = 128
 PACK = 4
-KP = 512
-NB = 128
-NQ = 256
-SQUARE_ON_VECTOR = (3, 5, 7)
-GS = 512
+PASS = P * PACK
+BANK = 512
+KIB = 1024
+BLOCK = BANK // PACK
+QUARTER = BANK // 2
+BLOCKS = S // BLOCK
+QUARTERS = S // QUARTER
+SLICE = 512
+AHEAD = 6
+SQUARE_ON_VECTOR = (3, 5)
 
 
 def tile_list_stone_seating_scores_kernel(
@@ -31,11 +36,22 @@ def tile_list_stone_seating_scores_kernel(
     nc = tc.nc
     with ExitStack() as ctx:
         keep = ctx.enter_context(tc.tile_pool(name="keep", bufs=1))
-        ring = ctx.enter_context(tc.tile_pool(name="ring", bufs=3))
+        ring = ctx.enter_context(tc.tile_pool(name="ring", bufs=2 * QUARTERS))
+        shared = ctx.enter_context(tc.tile_pool(name="shared", bufs=1))
         psum = ctx.enter_context(tc.psum_pool(name="psum", bufs=8))
 
-        def held(name, shape, dtype, tag=None):
-            return keep.tile(shape, dtype, name=name, tag=tag or name, align_bytes=64)
+        def held(name, shape, dtype):
+            return keep.tile(shape, dtype, name=name, align_bytes=64)
+
+        def placed(name, shape, dtype, offset):
+            return shared.tile(shape, dtype, name=name, align_bytes=64, offset=offset)
+
+        raw01_at, raw11_at, raw3_at, bf3_at = 0, 8 * KIB, 16 * KIB, 24 * KIB
+        codes_at = {("h0", q): raw3_at + q * KIB for q in range(1, QUARTERS)}
+        codes_at.update({("h2", q): raw3_at + (3 + q) * KIB for q in range(1, QUARTERS)})
+        codes_at["h0", 0] = raw11_at
+        codes_at["h2", 0] = raw01_at
+        v2_late_at = (raw3_at, bf3_at)
 
         list1 = keep.tile([P, S // 16], U16, name="list1")
         list2 = keep.tile([P, S2 // 16], U16, name="list2")
@@ -46,94 +62,108 @@ def tile_list_stone_seating_scores_kernel(
         v_s1 = held("v_s1", [P, S], U8)
         v2_0 = held("v2_0", [P, S2], U32)
         v2_s = held("v2_s", [P, S2], U8)
-        w2_raw = held("w2_raw", [P, 2 * H // 2], U32)
-        w2_c = held("w2_c", [P, 2 * H // 2], U32)
-        w2_sraw = held("w2_sraw", [P, 2 * H // 4], U32)
-        w2_s = held("w2_s", [P, 2 * H // 4], U32)
+        w2_raw = held("w2_raw", [P, H], U32)
+        w2_c = held("w2_c", [P, H], U32)
+        w2_sraw = held("w2_sraw", [P, H // 2], U32)
+        w2_s = held("w2_s", [P, H // 2], U32)
         w1_raw = {}
         w1_c = {}
         w1_s = {}
         for b in range(2):
             for a in range(2):
-                w1_raw[a, b] = held("w1_raw%d%d" % (a, b), [P, PACK, KP], F32)
-                w1_c[a, b] = held("w1_c%d%d" % (a, b), [P, KP], U32)
-                w1_s[a, b] = held("w1_s%d%d" % (a, b), [P, KP], U8)
-        w3_raw = held("w3_raw", [P, PACK, S2], F32)
+                if b == 0:
+                    w1_raw[a, b] = held("w1_raw%d%d" % (a, b), [P, PACK, PASS], F32)
+                else:
+                    w1_raw[a, b] = placed("w1_raw%d%d" % (a, b), [P, PACK, PASS], F32, (raw01_at, raw11_at)[a])
+                w1_c[a, b] = held("w1_c%d%d" % (a, b), [P, PASS], U32)
+                w1_s[a, b] = held("w1_s%d%d" % (a, b), [P, PASS], U8)
+        w3_raw = placed("w3_raw", [P, PACK, S2], F32, raw3_at)
         w3_c = held("w3_c", [P, S2], U32)
         w3_s = held("w3_s", [P, S2], U8)
-        names = ("h0", "h1", "h2")
-        h_bf = {n: held(n + "_bf", [P, PACK * S], BF16) for n in names}
-        h_c = {"h1": held("h1_c", [P, S], U32)}
+        results = ("h0", "h1", "h2")
+        h_bf = {name: held(name + "_bf", [P, PACK * S], BF16) for name in results}
+        h_s = {name: held(name + "_s", [P, S], U8) for name in results}
+        h_c = {}
         v2_1 = {}
-        h_s = {n: held(n + "_s", [P, S], U8) for n in names}
 
-        nc.vector.memset(tab_s[:].bitcast(I32), 0)
+        warm_in = held("warm_in", [P, 1], F32)
+        warm_out = held("warm_out", [P, 1], F32)
+        nc.gpsimd.memset(warm_in[:], 1.0)
+        nc.scalar.activation(out=warm_out[:], in_=warm_in[:], func=ACT.Abs_reciprocal_sqrt, bias=1.0)
+
+        tab_s32 = tab_s[:].bitcast(I32)
+        nc.vector.memset(tab_s32[:, 0 : T // 8], 0)
+        nc.gpsimd.memset(tab_s32[:, T // 8 : T // 4], 0)
         nc.vector.memset(v_s1[:].bitcast(I32), 0)
         nc.vector.memset(w2_s[:].bitcast(I32), 0)
-        for q in range(2):
-            for a in range(2):
-                nc.scalar.dma_start(
-                    out=tab_s[32 * q + 4 * a : 32 * q + 4 * a + 4, :].bitcast(I32),
-                    in_=tab_scales[a, 4 * q : 4 * q + 4, :].bitcast(I32),
-                )
-        for q in range(2, 4):
-            nc.gpsimd.dma_start(
-                out=tab_s[32 * q : 32 * q + 8, :].bitcast(I32),
-                in_=tab_scales[:, 4 * q : 4 * q + 4, :].bitcast(I32),
-            )
 
-        def load_tab(a):
+        def load_words(a):
             nc.sync.dma_start(
                 out=tab[a][:].bitcast(I32), in_=tab_words[a].rearrange("p n t -> p (n t)").bitcast(I32)
             )
 
         nc.sync.dma_start(list1[:], offs)
-        nc.sync.dma_start(list2[:], offs2)
         nc.sync.dma_start(
             out=w2_raw[:].bitcast(I32).rearrange("p (a n) -> p a n", a=2),
             in_=w2_words.bitcast(I32).rearrange("a p n -> p a n"),
         )
-        for q in range(4):
-            nc.gpsimd.dma_start(
-                out=w2_sraw[32 * q : 32 * q + 4, :].bitcast(I32).rearrange("p (a n) -> p a n", a=2),
-                in_=w2_scales[:, 4 * q : 4 * q + 4, :].bitcast(I32).rearrange("a r n -> r a n"),
+        for low in range(2):
+            high = low + 2
+            nc.sync.dma_start(
+                out=tab_s32[32 * high : 32 * high + 8, :],
+                in_=tab_scales[:, 4 * high : 4 * high + 4, :].bitcast(I32),
             )
-        load_tab(0)
-        load_tab(1)
+            for a in range(2):
+                nc.sync.dma_start(
+                    out=tab_s32[32 * low + 4 * a : 32 * low + 4 * a + 4, :],
+                    in_=tab_scales[a, 4 * low : 4 * low + 4, :].bitcast(I32),
+                )
+        load_words(0)
+        nc.sync.dma_start(list2[:], offs2)
+        for quad in range(4):
+            nc.sync.dma_start(
+                out=w2_sraw[32 * quad : 32 * quad + 4, :].bitcast(I32).rearrange("p (a n) -> p a n", a=2),
+                in_=w2_scales[:, 4 * quad : 4 * quad + 4, :].bitcast(I32).rearrange("a r n -> r a n"),
+            )
+        load_words(1)
+        nc.vector.tensor_copy(v_s[:], tab_s[:].indirect(list1[:]))
+        for row in range(4):
+            nc.sync.dma_start(out=v_s1[row:P:32, :].bitcast(I32), in_=v_s[4 + row : P : 32, :].bitcast(I32))
         for b in range(2):
             for a in range(2):
                 nc.sync.dma_start(
                     out=w1_raw[a, b][:],
-                    in_=w1[KP * a : KP * (a + 1), KP * b : KP * (b + 1)].rearrange("(p j) c -> p j c", j=PACK),
+                    in_=w1[PASS * a : PASS * (a + 1), PASS * b : PASS * (b + 1)].rearrange(
+                        "(p j) c -> p j c", j=PACK
+                    ),
                 )
-        w3_rows = w3.rearrange("(g t q) m -> t g q m", t=PACK, q=8)
-        for t in range(PACK):
-            nc.sync.dma_start(out=w3_raw[:, t, :], in_=w3_rows[t])
+        w3_rows = w3.rearrange("(g i q) m -> i g q m", i=PACK, q=8)
+        for i in range(PACK):
+            nc.sync.dma_start(out=w3_raw[:, i, :], in_=w3_rows[i])
 
-        def gather_words(a):
-            for s0 in range(0, S, GS):
+        def gather_v(a):
+            for s0 in range(0, S, SLICE):
                 nc.vector.tensor_copy(
-                    v[a][:, s0 : s0 + GS], tab[a][:].indirect(list1[:, s0 // 16 : (s0 + GS) // 16])
+                    v[a][:, s0 : s0 + SLICE], tab[a][:].indirect(list1[:, s0 // 16 : (s0 + SLICE) // 16])
                 )
 
-        nc.vector.tensor_copy(v_s[:], tab_s[:].indirect(list1[:]))
-        for r in range(4):
-            nc.scalar.dma_start(
-                out=v_s1[r:P:32, :].bitcast(I32), in_=v_s[4 + r : P : 32, :].bitcast(I32)
-            )
+        def gather_v2_1(half):
+            v2_1[half] = placed("v2_1%d" % half, [P, 2 * P], U32, v2_late_at[half])
+            nc.vector.tensor_copy(v2_1[half][:], tab[1][:].indirect(list2[:, 16 * half : 16 * (half + 1)]))
+
         nc.vector.tensor_copy(v2_s[:], tab_s[:].indirect(list2[:]))
-        gather_words(0)
+        gather_v(0)
         nc.vector.tensor_copy(v2_0[:], tab[0][:].indirect(list2[:]))
 
         nc.scalar.copy(
-            out=w2_c[:].rearrange("p (a t g w) -> p a t g w", a=2, t=PACK, w=4),
-            in_=w2_raw[:].rearrange("p (a g t w) -> p a t g w", a=2, t=PACK, w=4),
+            out=w2_c[:].rearrange("p (a i g w) -> p a i g w", a=2, i=PACK, w=4),
+            in_=w2_raw[:].rearrange("p (a g i w) -> p a i g w", a=2, i=PACK, w=4),
         )
-        for q in range(4):
-            rows = slice(32 * q, 32 * q + 4)
+        for quad in range(4):
+            rows = slice(32 * quad, 32 * quad + 4)
             nc.scalar.copy(
-                out=w2_s[rows, :].rearrange("p (a t g w) -> p a t g w", a=2, t=PACK, w=2),
-                in_=w2_sraw[rows, :].rearrange("p (a g t w) -> p a t g w", a=2, t=PACK, w=2),
+                out=w2_s[rows, :].rearrange("p (a i g w) -> p a i g w", a=2, i=PACK, w=2),
+                in_=w2_sraw[rows, :].rearrange("p (a g i w) -> p a i g w", a=2, i=PACK, w=2),
             )
         w2_c8 = w2_c[:].bitcast(U8)
         w2_s8 = w2_s[:].bitcast(U8)
@@ -142,54 +172,80 @@ def tile_list_stone_seating_scores_kernel(
             nc.vector.quantize_mx(out=codes.bitcast(E4M3), scales=scales, in_=values)
 
         def prepare_w1(a, b):
-            g = held("w1_bf%d%d" % (a, b), [P, PACK * KP], BF16)
-            nc.vector.tensor_copy(
-                out=g[:].rearrange("p (t m j) -> p m j t", t=PACK, j=PACK),
-                in_=w1_raw[a, b][:].rearrange("p j (m t) -> p m j t", t=PACK),
-            )
-            return g
+            rounded = held("w1_bf%d%d" % (a, b), [P, PACK * PASS], BF16)
+            for i0 in (0, 2):
+                nc.vector.tensor_copy(
+                    out=rounded[:, PASS * i0 : PASS * (i0 + 2)].rearrange("p (i c j) -> p c i j", i=2, j=PACK),
+                    in_=w1_raw[a, b][:].rearrange("p j (c i) -> p c i j", i=PACK)[:, :, i0 : i0 + 2, :],
+                )
+            for i0 in (0, 2):
+                words = slice(P * i0, P * (i0 + 2))
+                quantise(w1_c[a, b][:, words], w1_s[a, b][:, words], rounded[:, PASS * i0 : PASS * (i0 + 2)])
 
-        def first_pass(name, a, jb, bank):
-            cols = slice(NB * jb, NB * (jb + 1))
-            for t in range(PACK):
+        def prepare_w3():
+            rounded = placed("w3_bf", [P, PACK * S2], BF16, bf3_at)
+            halves = [slice(m0, m0 + S2 // 2) for m0 in (0, S2 // 2)]
+            for m in halves:
+                nc.vector.tensor_scalar(
+                    out=rounded[:, PACK * m.start : PACK * m.stop].rearrange("p (c n i) -> p c i n", n=4, i=PACK),
+                    in0=w3_raw[:, :, m].rearrange("p i (c n) -> p c i n", n=4),
+                    scalar1=-1.0,
+                    scalar2=None,
+                    op0=ALU.mult,
+                )
+            for m in halves:
+                quantise(w3_c[:, m], w3_s[:, m], rounded[:, PACK * m.start : PACK * m.stop])
+
+        def new_bank():
+            return psum.tile([P, BANK], F32, name="bank")
+
+        def first_stage_pass(name, a, block, bank):
+            cols = slice(BLOCK * block, BLOCK * (block + 1))
+            for i in range(PACK):
                 if name == "h2":
-                    c0 = a * H + t * P
+                    c0 = a * H + i * P
                     lhs = w2_c8[:, 2 * c0 : 2 * (c0 + P)].bitcast(E2M1)
                     lhs_s = w2_s8[:, c0 : c0 + P]
                     rhs_s = (v_s, v_s1)[a][:, cols]
                 else:
-                    b = names.index(name)
-                    lhs = w1_c[a, b][:, t * P : (t + 1) * P].bitcast(E4M3)
-                    lhs_s = w1_s[a, b][:, t * P : (t + 1) * P]
+                    b = results.index(name)
+                    lhs = w1_c[a, b][:, i * P : (i + 1) * P].bitcast(E4M3)
+                    lhs_s = w1_s[a, b][:, i * P : (i + 1) * P]
                     rhs_s = v_s[4 * a : P, cols]
                 nc.tensor.matmul_mx(
-                    out=bank[:, t * NB : (t + 1) * NB],
+                    out=bank[:, i * BLOCK : (i + 1) * BLOCK],
                     lhsT=lhs,
                     lhsT_scale=lhs_s,
                     rhs=v[a][:, cols].bitcast(E4M3),
                     rhs_scale=rhs_s,
-                    start=(a == 0 and t == 0),
-                    stop=(a == 1 and t == PACK - 1),
+                    start=(a == 0 and i == 0),
+                    stop=(a == 1 and i == PACK - 1),
                 )
 
-        def empty_first(name, jb, bank):
+        def close_first_stage(name, block, bank):
+            first_stage_pass(name, 1, block, bank)
             nc.scalar.activation(
-                out=h_bf[name][:, PACK * NB * jb : PACK * NB * (jb + 1)].rearrange("p (n t) -> p n t", t=PACK),
-                in_=bank[:].rearrange("p (t n) -> p n t", t=PACK),
+                out=h_bf[name][:, BANK * block : BANK * (block + 1)].rearrange("p (c n i) -> p c i n", n=2, i=PACK),
+                in_=bank[:].rearrange("p (i c n) -> p c i n", n=2, i=PACK),
                 func=ACT.Relu if name == "h2" else ACT.Abs,
             )
 
-        def quantise_h(name, q):
-            cols = slice(NQ * q, NQ * (q + 1))
-            quantise(h_c[name][:, cols], h_s[name][:, cols], h_bf[name][:, PACK * NQ * q : PACK * NQ * (q + 1)])
-
-        def new_bank():
-            return psum.tile([P, 512], F32, name="bank")
+        def quantise_result(name, q):
+            if name == "h1":
+                h_c[name, q] = held("h1_c%d" % q, [P, QUARTER], U32)
+            else:
+                h_c[name, q] = placed("%s_c%d" % (name, q), [P, QUARTER], U32, codes_at[name, q])
+            quantise(
+                h_c[name, q][:],
+                h_s[name][:, QUARTER * q : QUARTER * (q + 1)],
+                h_bf[name][:, PACK * QUARTER * q : PACK * QUARTER * (q + 1)],
+            )
 
         def second_stage(q, half):
-            cols = slice(NQ * q, NQ * (q + 1))
+            cols = slice(QUARTER * q, QUARTER * (q + 1))
             bank = new_bank()
-            for i, name in enumerate(names):
+            order = ("h0", "h2", "h1")
+            for name in order:
                 for u in range(2):
                     m = slice(P * (2 * half + u), P * (2 * half + u + 1))
                     if name == "h2":
@@ -199,91 +255,77 @@ def tile_list_stone_seating_scores_kernel(
                     else:
                         lhs, lhs_s = v2_1[half][:, P * u : P * (u + 1)], v2_s[4:P, m]
                     nc.tensor.matmul_mx(
-                        out=bank[:, u * NQ : (u + 1) * NQ],
+                        out=bank[:, u * QUARTER : (u + 1) * QUARTER],
                         lhsT=lhs.bitcast(E4M3),
                         lhsT_scale=lhs_s,
-                        rhs=h_c[name][:, cols].bitcast(E4M3),
+                        rhs=h_c[name, q][:].bitcast(E4M3),
                         rhs_scale=h_s[name][:, cols],
-                        start=(i == 0 and u == 0),
-                        stop=(i == 2 and u == 1),
+                        start=(name == order[0] and u == 0),
+                        stop=(name == order[-1] and u == 1),
                     )
-            y = ring.tile([P, 512], F32, name="y")
+            square = ring.tile([P, BANK], F32, name="square")
+            root = ring.tile([P, BANK], F32, name="root")
+            score = ring.tile([P, BANK], F32, name="score")
             if 2 * q + half in SQUARE_ON_VECTOR:
-                d = ring.tile([P, 512], F32, name="d")
-                nc.vector.tensor_copy(d[:], bank[:])
-                nc.vector.tensor_tensor(y[:], bank[:], d[:], ALU.mult)
+                diff = ring.tile([P, BANK], F32, name="diff", bufs=len(SQUARE_ON_VECTOR))
+                nc.vector.tensor_copy(diff[:], bank[:])
+                nc.vector.tensor_tensor(square[:], bank[:], diff[:], ALU.mult)
             else:
-                nc.scalar.activation(out=y[:], in_=bank[:], func=ACT.Square)
-            r = ring.tile([P, 512], F32, name="r")
-            nc.scalar.activation(out=r[:], in_=y[:], func=ACT.Abs_reciprocal_sqrt, bias=1.0)
-            res = ring.tile([P, 512], F32, name="res")
-            nc.vector.tensor_tensor(res[:], r[:], r[:], ALU.mult)
-            nc.sync.dma_start(
-                out=out[2 * P * half : 2 * P * (half + 1), cols].rearrange("(u p) j -> p u j", u=2),
-                in_=res[:].rearrange("p (u j) -> p u j", u=2),
-            )
+                nc.scalar.activation(out=square[:], in_=bank[:], func=ACT.Square)
+            last = q == QUARTERS - 1 and half == 1
+            for u0, u1 in ((0, 1), (1, 2)) if last else ((0, 2),):
+                part = slice(u0 * QUARTER, u1 * QUARTER)
+                nc.scalar.activation(
+                    out=root[:, part], in_=square[:, part], func=ACT.Abs_reciprocal_sqrt, bias=1.0
+                )
+                nc.vector.tensor_tensor(score[:, part], root[:, part], root[:, part], ALU.mult)
+                rows = slice(P * (2 * half + u0), P * (2 * half + u1))
+                nc.sync.dma_start(
+                    out=out[rows, cols].rearrange("(u p) j -> p u j", p=P),
+                    in_=score[:, part].rearrange("p (u j) -> p u j", j=QUARTER),
+                )
 
-        nblk = S // NB
-        banks = [new_bank() for jb in range(nblk)]
-        for jb in range(nblk):
-            first_pass("h2", 0, jb, banks[jb])
-        gather_words(1)
-        for jb in range(nblk):
-            first_pass("h2", 1, jb, banks[jb])
-            empty_first("h2", jb, banks[jb])
+        banks = [new_bank() for block in range(BLOCKS)]
+        for block in range(BLOCKS):
+            first_stage_pass("h2", 0, block, banks[block])
+        gather_v(1)
+        for block in range(BLOCKS):
+            close_first_stage("h2", block, banks[block])
 
-        def gather_v2_1(half, tag):
-            v2_1[half] = held("v2_1%d" % half, [P, 2 * P], U32, tag=tag)
-            nc.vector.tensor_copy(v2_1[half][:], tab[1][:].indirect(list2[:, 16 * half : 16 * (half + 1)]))
+        prepare_w1(0, 0)
+        prepare_w1(1, 0)
+        banks = [new_bank() for block in range(BLOCKS)]
+        for block in range(BLOCKS):
+            first_stage_pass("h0", 0, block, banks[block])
+        for block in range(BLOCKS):
+            close_first_stage("h0", block, banks[block])
 
-        g00 = prepare_w1(0, 0)
-        quantise(w1_c[0, 0][:], w1_s[0, 0][:], g00[:])
-        g10 = prepare_w1(1, 0)
-        quantise(w1_c[1, 0][:], w1_s[1, 0][:], g10[:])
-        gather_v2_1(0, "w1_raw10")
+        prepare_w1(0, 1)
+        quantise_result("h2", 0)
+        prepare_w1(1, 1)
+        prepare_w3()
 
-        banks = [new_bank() for jb in range(nblk)]
-        for jb in range(nblk):
-            first_pass("h0", 0, jb, banks[jb])
-        for jb in range(nblk):
-            first_pass("h0", 1, jb, banks[jb])
-            empty_first("h0", jb, banks[jb])
-
-        g01 = prepare_w1(0, 1)
-        quantise(w1_c[0, 1][:], w1_s[0, 1][:], g01[:])
-        gather_v2_1(1, "w1_raw01")
-        g11 = prepare_w1(1, 1)
-        quantise(w1_c[1, 1][:], w1_s[1, 1][:], g11[:])
-        g3 = held("w3_bf", [P, PACK * S2], BF16)
-        nc.vector.tensor_scalar(
-            out=g3[:].rearrange("p (c i t) -> p c t i", i=4, t=PACK),
-            in0=w3_raw[:].rearrange("p t (c i) -> p c t i", i=4),
-            scalar1=-1.0,
-            scalar2=None,
-            op0=ALU.mult,
-        )
-        quantise(w3_c[:], w3_s[:], g3[:])
-        h_c["h0"] = held("h0_c", [P, S], U32, tag="w1_raw11")
-        h_c["h2"] = held("h2_c", [P, S], U32, tag="w1_bf11")
-        for q in range(4):
-            quantise_h("h0", q)
-            quantise_h("h2", q)
-
-        ahead = 6
         banks = {}
-        for jb in range(ahead):
-            banks[jb] = new_bank()
-            first_pass("h1", 0, jb, banks[jb])
-        for q in range(4):
-            for jb in (2 * q, 2 * q + 1):
-                if jb >= ahead:
-                    banks[jb] = new_bank()
-                    first_pass("h1", 0, jb, banks[jb])
-                first_pass("h1", 1, jb, banks[jb])
-                empty_first("h1", jb, banks[jb])
-            quantise_h("h1", q)
-            if q > 0:
-                second_stage(q - 1, 0)
-                second_stage(q - 1, 1)
-        second_stage(3, 0)
-        second_stage(3, 1)
+        for block in range(AHEAD):
+            banks[block] = new_bank()
+            first_stage_pass("h1", 0, block, banks[block])
+        for q in range(QUARTERS):
+            for block in (2 * q, 2 * q + 1):
+                if block >= AHEAD:
+                    banks[block] = new_bank()
+                    first_stage_pass("h1", 0, block, banks[block])
+                close_first_stage("h1", block, banks[block])
+            quantise_result("h0", q)
+            if q == 0:
+                gather_v2_1(0)
+            else:
+                quantise_result("h2", q)
+            quantise_result("h1", q)
+            if q == 0:
+                gather_v2_1(1)
+            if q == 1:
+                second_stage(0, 0)
+                second_stage(0, 1)
+        for q in range(1, QUARTERS):
+            second_stage(q, 0)
+            second_stage(q, 1)

from contextlib import ExitStack

import concourse.mybir as mybir

K, H, T, S, S2 = 1024, 512, 4096, 1024, 512
FLOPS = 2 * S * (K * K + S2 * K + K * H + H * S2)

F32 = mybir.dt.float32
BF16 = mybir.dt.bfloat16
I32 = mybir.dt.int32
U32 = mybir.dt.uint32
U16 = mybir.dt.uint16
U8 = mybir.dt.uint8
E4M3 = mybir.dt.float8_e4m3fn_x4
E2M1 = mybir.dt.float4_e2m1fn_x4
ACT = mybir.ActivationFunctionType
ALU = mybir.AluOpType

P = 128
PACK = 4
PASS = P * PACK
BANK = 512
KIB = 1024
BLOCK = BANK // PACK
QUARTER = BANK // 2
BLOCKS = S // BLOCK
QUARTERS = S // QUARTER
SLICE = 512
AHEAD = 6
SQUARE_ON_VECTOR = (3, 5)


def tile_list_stone_seating_scores_kernel(
    tc, tab_words, tab_scales, offs, offs2, w1, w2_words, w2_scales, w3, out
):
    nc = tc.nc
    with ExitStack() as ctx:
        keep = ctx.enter_context(tc.tile_pool(name="keep", bufs=1))
        ring = ctx.enter_context(tc.tile_pool(name="ring", bufs=2 * QUARTERS))
        shared = ctx.enter_context(tc.tile_pool(name="shared", bufs=1))
        psum = ctx.enter_context(tc.psum_pool(name="psum", bufs=8))

        def held(name, shape, dtype):
            return keep.tile(shape, dtype, name=name, align_bytes=64)

        def placed(name, shape, dtype, offset):
            return shared.tile(shape, dtype, name=name, align_bytes=64, offset=offset)

        raw01_at, raw11_at, raw3_at, bf3_at = 0, 8 * KIB, 16 * KIB, 24 * KIB
        codes_at = {("h0", q): raw3_at + q * KIB for q in range(1, QUARTERS)}
        codes_at.update({("h2", q): raw3_at + (3 + q) * KIB for q in range(1, QUARTERS)})
        codes_at["h0", 0] = raw11_at
        codes_at["h2", 0] = raw01_at
        v2_late_at = (raw3_at, bf3_at)

        list1 = keep.tile([P, S // 16], U16, name="list1")
        list2 = keep.tile([P, S2 // 16], U16, name="list2")
        tab = [held("tab%d" % a, [P, T], U32) for a in range(2)]
        tab_s = held("tab_s", [P, T], U8)
        v = [held("v%d" % a, [P, S], U32) for a in range(2)]
        v_s = held("v_s", [P, S], U8)
        v_s1 = held("v_s1", [P, S], U8)
        v2_0 = held("v2_0", [P, S2], U32)
        v2_s = held("v2_s", [P, S2], U8)
        w2_raw = held("w2_raw", [P, H], U32)
        w2_c = held("w2_c", [P, H], U32)
        w2_sraw = held("w2_sraw", [P, H // 2], U32)
        w2_s = held("w2_s", [P, H // 2], U32)
        w1_raw = {}
        w1_c = {}
        w1_s = {}
        for b in range(2):
            for a in range(2):
                if b == 0:
                    w1_raw[a, b] = held("w1_raw%d%d" % (a, b), [P, PACK, PASS], F32)
                else:
                    w1_raw[a, b] = placed("w1_raw%d%d" % (a, b), [P, PACK, PASS], F32, (raw01_at, raw11_at)[a])
                w1_c[a, b] = held("w1_c%d%d" % (a, b), [P, PASS], U32)
                w1_s[a, b] = held("w1_s%d%d" % (a, b), [P, PASS], U8)
        w3_raw = placed("w3_raw", [P, PACK, S2], F32, raw3_at)
        w3_c = held("w3_c", [P, S2], U32)
        w3_s = held("w3_s", [P, S2], U8)
        results = ("h0", "h1", "h2")
        h_bf = {name: held(name + "_bf", [P, PACK * S], BF16) for name in results}
        h_s = {name: held(name + "_s", [P, S], U8) for name in results}
        h_c = {}
        v2_1 = {}

        warm_in = held("warm_in", [P, 1], F32)
        warm_out = held("warm_out", [P, 1], F32)
        nc.gpsimd.memset(warm_in[:], 1.0)
        nc.scalar.activation(out=warm_out[:], in_=warm_in[:], func=ACT.Abs_reciprocal_sqrt, bias=1.0)

        tab_s32 = tab_s[:].bitcast(I32)
        nc.vector.memset(tab_s32[:, 0 : T // 8], 0)
        nc.gpsimd.memset(tab_s32[:, T // 8 : T // 4], 0)
        nc.vector.memset(v_s1[:].bitcast(I32), 0)
        nc.vector.memset(w2_s[:].bitcast(I32), 0)

        def load_words(a):
            nc.sync.dma_start(
                out=tab[a][:].bitcast(I32), in_=tab_words[a].rearrange("p n t -> p (n t)").bitcast(I32)
            )

        nc.sync.dma_start(list1[:], offs)
        nc.sync.dma_start(
            out=w2_raw[:].bitcast(I32).rearrange("p (a n) -> p a n", a=2),
            in_=w2_words.bitcast(I32).rearrange("a p n -> p a n"),
        )
        for low in range(2):
            high = low + 2
            nc.sync.dma_start(
                out=tab_s32[32 * high : 32 * high + 8, :],
                in_=tab_scales[:, 4 * high : 4 * high + 4, :].bitcast(I32),
            )
            for a in range(2):
                nc.sync.dma_start(
                    out=tab_s32[32 * low + 4 * a : 32 * low + 4 * a + 4, :],
                    in_=tab_scales[a, 4 * low : 4 * low + 4, :].bitcast(I32),
                )
        load_words(0)
        nc.sync.dma_start(list2[:], offs2)
        for quad in range(4):
            nc.sync.dma_start(
                out=w2_sraw[32 * quad : 32 * quad + 4, :].bitcast(I32).rearrange("p (a n) -> p a n", a=2),
                in_=w2_scales[:, 4 * quad : 4 * quad + 4, :].bitcast(I32).rearrange("a r n -> r a n"),
            )
        load_words(1)
        nc.vector.tensor_copy(v_s[:], tab_s[:].indirect(list1[:]))
        for row in range(4):
            nc.sync.dma_start(out=v_s1[row:P:32, :].bitcast(I32), in_=v_s[4 + row : P : 32, :].bitcast(I32))
        for b in range(2):
            for a in range(2):
                nc.sync.dma_start(
                    out=w1_raw[a, b][:],
                    in_=w1[PASS * a : PASS * (a + 1), PASS * b : PASS * (b + 1)].rearrange(
                        "(p j) c -> p j c", j=PACK
                    ),
                )
        w3_rows = w3.rearrange("(g i q) m -> i g q m", i=PACK, q=8)
        for i in range(PACK):
            nc.sync.dma_start(out=w3_raw[:, i, :], in_=w3_rows[i])

        def gather_v(a):
            for s0 in range(0, S, SLICE):
                nc.vector.tensor_copy(
                    v[a][:, s0 : s0 + SLICE], tab[a][:].indirect(list1[:, s0 // 16 : (s0 + SLICE) // 16])
                )

        def gather_v2_1(half):
            v2_1[half] = placed("v2_1%d" % half, [P, 2 * P], U32, v2_late_at[half])
            nc.vector.tensor_copy(v2_1[half][:], tab[1][:].indirect(list2[:, 16 * half : 16 * (half + 1)]))

        nc.vector.tensor_copy(v2_s[:], tab_s[:].indirect(list2[:]))
        gather_v(0)
        nc.vector.tensor_copy(v2_0[:], tab[0][:].indirect(list2[:]))

        nc.scalar.copy(
            out=w2_c[:].rearrange("p (a i g w) -> p a i g w", a=2, i=PACK, w=4),
            in_=w2_raw[:].rearrange("p (a g i w) -> p a i g w", a=2, i=PACK, w=4),
        )
        for quad in range(4):
            rows = slice(32 * quad, 32 * quad + 4)
            nc.scalar.copy(
                out=w2_s[rows, :].rearrange("p (a i g w) -> p a i g w", a=2, i=PACK, w=2),
                in_=w2_sraw[rows, :].rearrange("p (a g i w) -> p a i g w", a=2, i=PACK, w=2),
            )
        w2_c8 = w2_c[:].bitcast(U8)
        w2_s8 = w2_s[:].bitcast(U8)

        def quantise(codes, scales, values):
            nc.vector.quantize_mx(out=codes.bitcast(E4M3), scales=scales, in_=values)

        def prepare_w1(a, b):
            rounded = held("w1_bf%d%d" % (a, b), [P, PACK * PASS], BF16)
            for i0 in (0, 2):
                nc.vector.tensor_copy(
                    out=rounded[:, PASS * i0 : PASS * (i0 + 2)].rearrange("p (i c j) -> p c i j", i=2, j=PACK),
                    in_=w1_raw[a, b][:].rearrange("p j (c i) -> p c i j", i=PACK)[:, :, i0 : i0 + 2, :],
                )
            for i0 in (0, 2):
                words = slice(P * i0, P * (i0 + 2))
                quantise(w1_c[a, b][:, words], w1_s[a, b][:, words], rounded[:, PASS * i0 : PASS * (i0 + 2)])

        def prepare_w3():
            rounded = placed("w3_bf", [P, PACK * S2], BF16, bf3_at)
            halves = [slice(m0, m0 + S2 // 2) for m0 in (0, S2 // 2)]
            for m in halves:
                nc.vector.tensor_scalar(
                    out=rounded[:, PACK * m.start : PACK * m.stop].rearrange("p (c n i) -> p c i n", n=4, i=PACK),
                    in0=w3_raw[:, :, m].rearrange("p i (c n) -> p c i n", n=4),
                    scalar1=-1.0,
                    scalar2=None,
                    op0=ALU.mult,
                )
            for m in halves:
                quantise(w3_c[:, m], w3_s[:, m], rounded[:, PACK * m.start : PACK * m.stop])

        def new_bank():
            return psum.tile([P, BANK], F32, name="bank")

        def first_stage_pass(name, a, block, bank):
            cols = slice(BLOCK * block, BLOCK * (block + 1))
            for i in range(PACK):
                if name == "h2":
                    c0 = a * H + i * P
                    lhs = w2_c8[:, 2 * c0 : 2 * (c0 + P)].bitcast(E2M1)
                    lhs_s = w2_s8[:, c0 : c0 + P]
                    rhs_s = (v_s, v_s1)[a][:, cols]
                else:
                    b = results.index(name)
                    lhs = w1_c[a, b][:, i * P : (i + 1) * P].bitcast(E4M3)
                    lhs_s = w1_s[a, b][:, i * P : (i + 1) * P]
                    rhs_s = v_s[4 * a : P, cols]
                nc.tensor.matmul_mx(
                    out=bank[:, i * BLOCK : (i + 1) * BLOCK],
                    lhsT=lhs,
                    lhsT_scale=lhs_s,
                    rhs=v[a][:, cols].bitcast(E4M3),
                    rhs_scale=rhs_s,
                    start=(a == 0 and i == 0),
                    stop=(a == 1 and i == PACK - 1),
                )

        def close_first_stage(name, block, bank):
            first_stage_pass(name, 1, block, bank)
            nc.scalar.activation(
                out=h_bf[name][:, BANK * block : BANK * (block + 1)].rearrange("p (c n i) -> p c i n", n=2, i=PACK),
                in_=bank[:].rearrange("p (i c n) -> p c i n", n=2, i=PACK),
                func=ACT.Relu if name == "h2" else ACT.Abs,
            )

        def quantise_result(name, q):
            if name == "h1":
                h_c[name, q] = held("h1_c%d" % q, [P, QUARTER], U32)
            else:
                h_c[name, q] = placed("%s_c%d" % (name, q), [P, QUARTER], U32, codes_at[name, q])
            quantise(
                h_c[name, q][:],
                h_s[name][:, QUARTER * q : QUARTER * (q + 1)],
                h_bf[name][:, PACK * QUARTER * q : PACK * QUARTER * (q + 1)],
            )

        def second_stage(q, half):
            cols = slice(QUARTER * q, QUARTER * (q + 1))
            bank = new_bank()
            order = ("h0", "h2", "h1")
            for name in order:
                for u in range(2):
                    m = slice(P * (2 * half + u), P * (2 * half + u + 1))
                    if name == "h2":
                        lhs, lhs_s = w3_c[:, m], w3_s[:, m]
                    elif name == "h0":
                        lhs, lhs_s = v2_0[:, m], v2_s[:, m]
                    else:
                        lhs, lhs_s = v2_1[half][:, P * u : P * (u + 1)], v2_s[4:P, m]
                    nc.tensor.matmul_mx(
                        out=bank[:, u * QUARTER : (u + 1) * QUARTER],
                        lhsT=lhs.bitcast(E4M3),
                        lhsT_scale=lhs_s,
                        rhs=h_c[name, q][:].bitcast(E4M3),
                        rhs_scale=h_s[name][:, cols],
                        start=(name == order[0] and u == 0),
                        stop=(name == order[-1] and u == 1),
                    )
            square = ring.tile([P, BANK], F32, name="square")
            root = ring.tile([P, BANK], F32, name="root")
            score = ring.tile([P, BANK], F32, name="score")
            if 2 * q + half in SQUARE_ON_VECTOR:
                diff = ring.tile([P, BANK], F32, name="diff", bufs=len(SQUARE_ON_VECTOR))
                nc.vector.tensor_copy(diff[:], bank[:])
                nc.vector.tensor_tensor(square[:], bank[:], diff[:], ALU.mult)
            else:
                nc.scalar.activation(out=square[:], in_=bank[:], func=ACT.Square)
            last = q == QUARTERS - 1 and half == 1
            for u0, u1 in ((0, 1), (1, 2)) if last else ((0, 2),):
                part = slice(u0 * QUARTER, u1 * QUARTER)
                nc.scalar.activation(
                    out=root[:, part], in_=square[:, part], func=ACT.Abs_reciprocal_sqrt, bias=1.0
                )
                nc.vector.tensor_tensor(score[:, part], root[:, part], root[:, part], ALU.mult)
                rows = slice(P * (2 * half + u0), P * (2 * half + u1))
                nc.sync.dma_start(
                    out=out[rows, cols].rearrange("(u p) j -> p u j", p=P),
                    in_=score[:, part].rearrange("p (u j) -> p u j", j=QUARTER),
                )

        banks = [new_bank() for block in range(BLOCKS)]
        for block in range(BLOCKS):
            first_stage_pass("h2", 0, block, banks[block])
        gather_v(1)
        for block in range(BLOCKS):
            close_first_stage("h2", block, banks[block])

        prepare_w1(0, 0)
        prepare_w1(1, 0)
        banks = [new_bank() for block in range(BLOCKS)]
        for block in range(BLOCKS):
            first_stage_pass("h0", 0, block, banks[block])
        for block in range(BLOCKS):
            close_first_stage("h0", block, banks[block])

        prepare_w1(0, 1)
        quantise_result("h2", 0)
        prepare_w1(1, 1)
        prepare_w3()

        banks = {}
        for block in range(AHEAD):
            banks[block] = new_bank()
            first_stage_pass("h1", 0, block, banks[block])
        for q in range(QUARTERS):
            for block in (2 * q, 2 * q + 1):
                if block >= AHEAD:
                    banks[block] = new_bank()
                    first_stage_pass("h1", 0, block, banks[block])
                close_first_stage("h1", block, banks[block])
            quantise_result("h0", q)
            if q == 0:
                gather_v2_1(0)
            else:
                quantise_result("h2", q)
            quantise_result("h1", q)
            if q == 0:
                gather_v2_1(1)
            if q == 1:
                second_stage(0, 0)
                second_stage(0, 1)
        for q in range(1, QUARTERS):
            second_stage(q, 0)
            second_stage(q, 1)
